import numpy as np
import ml_dtypes

BF16 = ml_dtypes.bfloat16


def bf(x):
    return np.asarray(x, np.float32).astype(BF16)


def f32(x):
    return np.asarray(x, np.float32)


def f64(x):
    return np.asarray(x).astype(np.float64)


def striped(idx):
    return np.tile(idx.reshape(-1, 16).T, (8, 1))


S, K, M, N, V, D = 1024, 128, 128, 1024, 64, 16


def setup_inputs():
    return {"table": bf(np.random.standard_normal((K, S))), "w": bf(2.0 * np.random.standard_normal((K, M)) / np.sqrt(K)), "r": f32(0.7 * np.random.standard_normal((1, N))), "offs": striped(np.random.permutation(np.tile(np.arange(S), 2))[:N])}


def reference(table, w, r, offs):
    idx = offs[:16].T.reshape(-1)
    x = f64(table)[:, idx]
    u = (f64(w).T @ x + f64(r)).reshape(M, V, D)
    u = u - u.max(axis=2, keepdims=True)
    return (u - np.log(np.exp(u).sum(axis=2, keepdims=True))).reshape(M, N)

@@ -1,0 +1,58 @@
+import concourse.mybir as mybir
+
+BF16, F32, U16 = mybir.dt.bfloat16, mybir.dt.float32, mybir.dt.uint16
+ALU = mybir.AluOpType
+ACT = mybir.ActivationFunctionType
+AXIS_X = mybir.AxisListType.X
+
+FLOPS = 2 * 128 * 128 * 1024
+
+SLATE = 16
+PIECE = 512
+
+
+def tile_rows_slate_logpr_rep_kernel(tc, table, w, r, offs, out):
+    nc = tc.nc
+    K, S = table.shape
+    M, N = out.shape
+    slates = PIECE // SLATE
+    with (
+        tc.tile_pool(name="held", bufs=1) as held,
+        tc.tile_pool(name="work", bufs=2) as work,
+        tc.psum_pool(name="psum", bufs=2) as psum,
+    ):
+        table_sb = held.tile([K, S], BF16)
+        w_sb = held.tile([K, M], BF16)
+        offsets = held.tile([128, N // 16], U16)
+        r_rows = held.tile([M, N], F32)
+        nc.sync.dma_start(table_sb[:], table)
+        nc.sync.dma_start(offsets[:], offs)
+        nc.scalar.dma_start(w_sb[:], w)
+        nc.scalar.dma_start(r_rows[:], r[0].partition_broadcast(M))
+
+        def by_slate(tile):
+            return tile[:].rearrange("p (v t) -> p v t", t=SLATE)
+
+        def per_slate(tile):
+            return tile[:].unsqueeze(2).to_broadcast([M, slates, SLATE])
+
+        for first in range(0, N, PIECE):
+            cols = slice(first, first + PIECE)
+            scores = psum.tile([M, PIECE], F32)
+            nc.tensor.matmul(scores[:], w_sb[:], table_sb[:].indirect(offsets[:, first // 16:(first + PIECE) // 16]),
+                             start=True, stop=True)
+            u = work.tile([M, PIECE], F32)
+            nc.vector.tensor_tensor(u[:], scores[:], r_rows[:, cols], ALU.add)
+            top = work.tile([M, slates], F32)
+            nc.vector.tensor_reduce(top[:], by_slate(u), AXIS_X, ALU.max)
+            shifted = work.tile([M, PIECE], F32)
+            nc.vector.tensor_tensor(by_slate(shifted), by_slate(u), per_slate(top), ALU.subtract)
+            exps = work.tile([M, PIECE], F32)
+            nc.scalar.activation(exps[:], shifted[:], ACT.Exp)
+            total = work.tile([M, slates], F32)
+            nc.vector.tensor_reduce(total[:], by_slate(exps), AXIS_X, ALU.add)
+            log_total = work.tile([M, slates], F32)
+            nc.scalar.activation(log_total[:], total[:], ACT.Ln)
+            result = work.tile([M, PIECE], F32)
+            nc.vector.tensor_tensor(by_slate(result), by_slate(shifted), per_slate(log_total), ALU.subtract)
+            nc.sync.dma_start(out[:, cols], result[:])

@@ -1,6 +1,8 @@
+import math
+
 import concourse.mybir as mybir
 
-BF16, F32, U16 = mybir.dt.bfloat16, mybir.dt.float32, mybir.dt.uint16
+BF16, F32, U16, U32 = mybir.dt.bfloat16, mybir.dt.float32, mybir.dt.uint16, mybir.dt.uint32
 ALU = mybir.AluOpType
 ACT = mybir.ActivationFunctionType
 AXIS_X = mybir.AxisListType.X
@@ -8,51 +10,94 @@ AXIS_X = mybir.AxisListType.X
 FLOPS = 2 * 128 * 128 * 1024
 
 SLATE = 16
-PIECE = 512
+PIECE = 256
+BATCH = 2
+
+LN2 = math.log(2.0)
+GAP = math.log(1.0 / LN2) - (1.0 / LN2 - 1.0) * LN2
+GUESS_SCALE = LN2 / 2.0 ** 23
+GUESS_BIAS = GAP / 2 - 127 * LN2
 
 
 def tile_rows_slate_logpr_rep_kernel(tc, table, w, r, offs, out):
     nc = tc.nc
     K, S = table.shape
     M, N = out.shape
+    pieces = N // PIECE
     slates = PIECE // SLATE
     with (
         tc.tile_pool(name="held", bufs=1) as held,
-        tc.tile_pool(name="work", bufs=2) as work,
-        tc.psum_pool(name="psum", bufs=2) as psum,
+        tc.tile_pool(name="work", bufs=pieces) as work,
+        tc.tile_pool(name="stats", bufs=pieces // BATCH) as stats,
+        tc.psum_pool(name="psum", bufs=pieces) as psum,
     ):
         table_sb = held.tile([K, S], BF16)
         w_sb = held.tile([K, M], BF16)
         offsets = held.tile([128, N // 16], U16)
-        r_rows = held.tile([M, N], F32)
+        r_twice = held.tile([2, N], F32)
         nc.sync.dma_start(table_sb[:], table)
         nc.sync.dma_start(offsets[:], offs)
         nc.scalar.dma_start(w_sb[:], w)
-        nc.scalar.dma_start(r_rows[:], r[0].partition_broadcast(M))
+        nc.scalar.dma_start(r_twice[:], r[0].partition_broadcast(2))
+
+        add_two_rows = held.tile([K, M], BF16)
+        nc.vector.memset(add_two_rows[:], 0.0)
+        nc.scalar.activation(add_two_rows[0:2, :], add_two_rows[0:2, :], ACT.Exp)
+        r_parts = held.tile([K, N], BF16)
+        nc.vector.memset(r_parts[:], 0.0)
+        take_off = held.tile([2, 1], F32)
+        nc.vector.memset(take_off[:], -1.0)
+        nc.vector.memset(take_off[0:1, :], 0.0)
+        r_rounded = held.tile([2, N], BF16)
+        for first in range(0, N, PIECE):
+            cols = slice(first, first + PIECE)
+            nc.scalar.activation(r_rounded[:, cols], r_twice[:, cols], ACT.Copy)
+            nc.vector.scalar_tensor_tensor(r_parts[0:2, cols], r_rounded[:, cols], take_off[:], r_twice[:, cols],
+                                           ALU.mult, ALU.add)
+
+        banks = [psum.tile([M, PIECE], F32, name="scores") for piece in range(pieces)]
+        for piece, scores in enumerate(banks):
+            entries = offsets[:, piece * PIECE // 16:(piece + 1) * PIECE // 16]
+            nc.tensor.matmul(scores[:], w_sb[:], table_sb[:].indirect(entries), start=True, stop=False)
+        for piece, scores in enumerate(banks):
+            nc.tensor.matmul(scores[:], add_two_rows[:], r_parts[:, piece * PIECE:(piece + 1) * PIECE],
+                             start=False, stop=True)
 
         def by_slate(tile):
             return tile[:].rearrange("p (v t) -> p v t", t=SLATE)
 
-        def per_slate(tile):
-            return tile[:].unsqueeze(2).to_broadcast([M, slates, SLATE])
+        def per_slate(values):
+            return values.unsqueeze(2).to_broadcast([M, slates, SLATE])
 
-        for first in range(0, N, PIECE):
-            cols = slice(first, first + PIECE)
-            scores = psum.tile([M, PIECE], F32)
-            nc.tensor.matmul(scores[:], w_sb[:], table_sb[:].indirect(offsets[:, first // 16:(first + PIECE) // 16]),
-                             start=True, stop=True)
-            u = work.tile([M, PIECE], F32)
-            nc.vector.tensor_tensor(u[:], scores[:], r_rows[:, cols], ALU.add)
-            top = work.tile([M, slates], F32)
-            nc.vector.tensor_reduce(top[:], by_slate(u), AXIS_X, ALU.max)
-            shifted = work.tile([M, PIECE], F32)
-            nc.vector.tensor_tensor(by_slate(shifted), by_slate(u), per_slate(top), ALU.subtract)
-            exps = work.tile([M, PIECE], F32)
-            nc.scalar.activation(exps[:], shifted[:], ACT.Exp)
-            total = work.tile([M, slates], F32)
-            nc.vector.tensor_reduce(total[:], by_slate(exps), AXIS_X, ALU.add)
-            log_total = work.tile([M, slates], F32)
-            nc.scalar.activation(log_total[:], total[:], ACT.Ln)
-            result = work.tile([M, PIECE], F32)
-            nc.vector.tensor_tensor(by_slate(result), by_slate(shifted), per_slate(log_total), ALU.subtract)
-            nc.sync.dma_start(out[:, cols], result[:])
+        for batch in range(pieces // BATCH):
+            total = stats.tile([M, BATCH * slates], F32)
+            shifted_tiles = []
+            for i in range(BATCH):
+                scores = banks[batch * BATCH + i]
+                top = work.tile([M, slates], F32)
+                nc.vector.tensor_reduce(top[:], by_slate(scores), AXIS_X, ALU.max)
+                shifted = work.tile([M, PIECE], F32)
+                nc.vector.tensor_tensor(by_slate(shifted), by_slate(scores), per_slate(top[:]), ALU.subtract)
+                exps = work.tile([M, PIECE], F32)
+                nc.scalar.activation(exps[:], shifted[:], ACT.Exp)
+                nc.vector.tensor_reduce(total[:, i * slates:(i + 1) * slates], by_slate(exps), AXIS_X, ALU.add)
+                shifted_tiles.append(shifted)
+
+            bits = total[:].bitcast(U32)
+            inverse = stats.tile([M, BATCH * slates], F32)
+            nc.scalar.activation(inverse[:], bits, ACT.Exp, scale=-GUESS_SCALE, bias=-GUESS_BIAS)
+            guess = stats.tile([M, BATCH * slates], F32)
+            nc.scalar.activation(guess[:], bits, ACT.Copy, scale=GUESS_SCALE, bias=GUESS_BIAS - 1.5)
+            ratio = stats.tile([M, BATCH * slates], F32)
+            nc.vector.tensor_tensor(ratio[:], total[:], inverse[:], ALU.mult)
+            parabola = stats.tile([M, BATCH * slates], F32)
+            nc.vector.scalar_tensor_tensor(parabola[:], ratio[:], -4.0, ratio[:], ALU.add, ALU.mult)
+            log_total = stats.tile([M, BATCH * slates], F32)
+            nc.vector.scalar_tensor_tensor(log_total[:], parabola[:], -0.5, guess[:], ALU.mult, ALU.add)
+
+            for i, shifted in enumerate(shifted_tiles):
+                first = (batch * BATCH + i) * PIECE
+                result = work.tile([M, PIECE], F32)
+                nc.vector.tensor_tensor(by_slate(result), by_slate(shifted),
+                                        per_slate(log_total[:, i * slates:(i + 1) * slates]), ALU.subtract)
+                nc.sync.dma_start(out[:, first:first + PIECE], result[:])

@@ -10,8 +10,7 @@ AXIS_X = mybir.AxisListType.X
 FLOPS = 2 * 128 * 128 * 1024
 
 SLATE = 16
-PIECE = 256
-BATCH = 2
+BATCHES = (((0, 256), (256, 512)), ((512, 768),), ((768, 1024),))
 
 LN2 = math.log(2.0)
 GAP = math.log(1.0 / LN2) - (1.0 / LN2 - 1.0) * LN2
@@ -23,13 +22,9 @@ def tile_rows_slate_logpr_rep_kernel(tc, table, w, r, offs, out):
     nc = tc.nc
     K, S = table.shape
     M, N = out.shape
-    pieces = N // PIECE
-    slates = PIECE // SLATE
     with (
         tc.tile_pool(name="held", bufs=1) as held,
-        tc.tile_pool(name="work", bufs=pieces) as work,
-        tc.tile_pool(name="stats", bufs=pieces // BATCH) as stats,
-        tc.psum_pool(name="psum", bufs=pieces) as psum,
+        tc.psum_pool(name="psum", bufs=1) as psum,
     ):
         table_sb = held.tile([K, S], BF16)
         w_sb = held.tile([K, M], BF16)
@@ -49,55 +44,56 @@ def tile_rows_slate_logpr_rep_kernel(tc, table, w, r, offs, out):
         nc.vector.memset(take_off[:], -1.0)
         nc.vector.memset(take_off[0:1, :], 0.0)
         r_rounded = held.tile([2, N], BF16)
-        for first in range(0, N, PIECE):
-            cols = slice(first, first + PIECE)
+        pieces = [slice(*piece) for batch in BATCHES for piece in batch]
+        for cols in pieces:
             nc.scalar.activation(r_rounded[:, cols], r_twice[:, cols], ACT.Copy)
             nc.vector.scalar_tensor_tensor(r_parts[0:2, cols], r_rounded[:, cols], take_off[:], r_twice[:, cols],
                                            ALU.mult, ALU.add)
 
-        banks = [psum.tile([M, PIECE], F32, name="scores") for piece in range(pieces)]
-        for piece, scores in enumerate(banks):
-            entries = offsets[:, piece * PIECE // 16:(piece + 1) * PIECE // 16]
-            nc.tensor.matmul(scores[:], w_sb[:], table_sb[:].indirect(entries), start=True, stop=False)
-        for piece, scores in enumerate(banks):
-            nc.tensor.matmul(scores[:], add_two_rows[:], r_parts[:, piece * PIECE:(piece + 1) * PIECE],
-                             start=False, stop=True)
+        banks = {cols.start: psum.tile([M, cols.stop - cols.start], F32, name="scores%d" % cols.start) for cols in pieces}
+        for cols in pieces:
+            entries = offsets[:, cols.start // 16:cols.stop // 16]
+            nc.tensor.matmul(banks[cols.start][:], w_sb[:], table_sb[:].indirect(entries), start=True, stop=False)
+        for cols in pieces:
+            nc.tensor.matmul(banks[cols.start][:], add_two_rows[:], r_parts[:, cols], start=False, stop=True)
 
-        def by_slate(tile):
-            return tile[:].rearrange("p (v t) -> p v t", t=SLATE)
+        def by_slate(values):
+            return values.rearrange("p (v t) -> p v t", t=SLATE)
 
-        def per_slate(values):
-            return values.unsqueeze(2).to_broadcast([M, slates, SLATE])
+        def per_slate(stat, cols):
+            values = stat[:, cols.start // SLATE:cols.stop // SLATE]
+            return values.unsqueeze(2).to_broadcast([M, (cols.stop - cols.start) // SLATE, SLATE])
 
-        for batch in range(pieces // BATCH):
-            total = stats.tile([M, BATCH * slates], F32)
-            shifted_tiles = []
-            for i in range(BATCH):
-                scores = banks[batch * BATCH + i]
-                top = work.tile([M, slates], F32)
-                nc.vector.tensor_reduce(top[:], by_slate(scores), AXIS_X, ALU.max)
-                shifted = work.tile([M, PIECE], F32)
-                nc.vector.tensor_tensor(by_slate(shifted), by_slate(scores), per_slate(top[:]), ALU.subtract)
-                exps = work.tile([M, PIECE], F32)
-                nc.scalar.activation(exps[:], shifted[:], ACT.Exp)
-                nc.vector.tensor_reduce(total[:, i * slates:(i + 1) * slates], by_slate(exps), AXIS_X, ALU.add)
-                shifted_tiles.append(shifted)
+        top = held.tile([M, N // SLATE], F32)
+        shifted = held.tile([M, N], F32)
+        exps = held.tile([M, N], F32)
+        total = held.tile([M, N // SLATE], F32)
+        inverse = held.tile([M, N // SLATE], F32)
+        guess = held.tile([M, N // SLATE], F32)
+        ratio = held.tile([M, N // SLATE], F32)
+        parabola = held.tile([M, N // SLATE], F32)
+        log_total = held.tile([M, N // SLATE], F32)
+        result = held.tile([M, N], F32)
+        for cols in pieces:
+            slates = slice(cols.start // SLATE, cols.stop // SLATE)
+            scores = by_slate(banks[cols.start][:])
+            nc.vector.tensor_reduce(top[:, slates], scores, AXIS_X, ALU.max)
+            nc.vector.tensor_tensor(by_slate(shifted[:, cols]), scores, per_slate(top, cols), ALU.subtract)
+            nc.scalar.activation(exps[:, cols], shifted[:, cols], ACT.Exp)
 
-            bits = total[:].bitcast(U32)
-            inverse = stats.tile([M, BATCH * slates], F32)
-            nc.scalar.activation(inverse[:], bits, ACT.Exp, scale=-GUESS_SCALE, bias=-GUESS_BIAS)
-            guess = stats.tile([M, BATCH * slates], F32)
-            nc.scalar.activation(guess[:], bits, ACT.Copy, scale=GUESS_SCALE, bias=GUESS_BIAS - 1.5)
-            ratio = stats.tile([M, BATCH * slates], F32)
-            nc.vector.tensor_tensor(ratio[:], total[:], inverse[:], ALU.mult)
-            parabola = stats.tile([M, BATCH * slates], F32)
-            nc.vector.scalar_tensor_tensor(parabola[:], ratio[:], -4.0, ratio[:], ALU.add, ALU.mult)
-            log_total = stats.tile([M, BATCH * slates], F32)
-            nc.vector.scalar_tensor_tensor(log_total[:], parabola[:], -0.5, guess[:], ALU.mult, ALU.add)
+        for batch in BATCHES:
+            cols = slice(batch[0][0], batch[-1][1])
+            slates = slice(cols.start // SLATE, cols.stop // SLATE)
+            nc.vector.tensor_reduce(total[:, slates], by_slate(exps[:, cols]), AXIS_X, ALU.add)
+            bits = total[:, slates].bitcast(U32)
+            nc.scalar.activation(inverse[:, slates], bits, ACT.Exp, scale=-GUESS_SCALE, bias=-GUESS_BIAS)
+            nc.scalar.activation(guess[:, slates], bits, ACT.Copy, scale=GUESS_SCALE, bias=GUESS_BIAS - 1.5)
+            nc.vector.tensor_tensor(ratio[:, slates], total[:, slates], inverse[:, slates], ALU.mult)
+            nc.vector.scalar_tensor_tensor(parabola[:, slates], ratio[:, slates], -4.0, ratio[:, slates], ALU.add, ALU.mult)
+            nc.vector.scalar_tensor_tensor(log_total[:, slates], parabola[:, slates], -0.5, guess[:, slates],
+                                           ALU.mult, ALU.add)
 
-            for i, shifted in enumerate(shifted_tiles):
-                first = (batch * BATCH + i) * PIECE
-                result = work.tile([M, PIECE], F32)
-                nc.vector.tensor_tensor(by_slate(result), by_slate(shifted),
-                                        per_slate(log_total[:, i * slates:(i + 1) * slates]), ALU.subtract)
-                nc.sync.dma_start(out[:, first:first + PIECE], result[:])
+        for cols in pieces:
+            nc.vector.tensor_tensor(by_slate(result[:, cols]), by_slate(shifted[:, cols]), per_slate(log_total, cols),
+                                    ALU.subtract)
+            nc.sync.dma_start(out[:, cols], result[:, cols])

@@ -46,7 +46,10 @@ def tile_rows_slate_logpr_rep_kernel(tc, table, w, r, offs, out):
         r_rounded = held.tile([2, N], BF16)
         pieces = [slice(*piece) for batch in BATCHES for piece in batch]
         for cols in pieces:
-            nc.scalar.activation(r_rounded[:, cols], r_twice[:, cols], ACT.Copy)
+            if cols.start == 0:
+                nc.vector.tensor_copy(r_rounded[:, cols], r_twice[:, cols])
+            else:
+                nc.scalar.activation(r_rounded[:, cols], r_twice[:, cols], ACT.Copy)
             nc.vector.scalar_tensor_tensor(r_parts[0:2, cols], r_rounded[:, cols], take_off[:], r_twice[:, cols],
                                            ALU.mult, ALU.add)
 
@@ -72,7 +75,7 @@ def tile_rows_slate_logpr_rep_kernel(tc, table, w, r, offs, out):
         guess = held.tile([M, N // SLATE], F32)
         ratio = held.tile([M, N // SLATE], F32)
         parabola = held.tile([M, N // SLATE], F32)
-        log_total = held.tile([M, N // SLATE], F32)
+        minus_log = held.tile([M, N // SLATE], F32)
         result = held.tile([M, N], F32)
         for cols in pieces:
             slates = slice(cols.start // SLATE, cols.stop // SLATE)
@@ -90,10 +93,16 @@ def tile_rows_slate_logpr_rep_kernel(tc, table, w, r, offs, out):
             nc.scalar.activation(guess[:, slates], bits, ACT.Copy, scale=GUESS_SCALE, bias=GUESS_BIAS - 1.5)
             nc.vector.tensor_tensor(ratio[:, slates], total[:, slates], inverse[:, slates], ALU.mult)
             nc.vector.scalar_tensor_tensor(parabola[:, slates], ratio[:, slates], -4.0, ratio[:, slates], ALU.add, ALU.mult)
-            nc.vector.scalar_tensor_tensor(log_total[:, slates], parabola[:, slates], -0.5, guess[:, slates],
-                                           ALU.mult, ALU.add)
+            nc.vector.scalar_tensor_tensor(minus_log[:, slates], parabola[:, slates], 0.5, guess[:, slates],
+                                           ALU.mult, ALU.subtract)
 
-        for cols in pieces:
-            nc.vector.tensor_tensor(by_slate(result[:, cols]), by_slate(shifted[:, cols]), per_slate(log_total, cols),
-                                    ALU.subtract)
+        for cols in pieces[1:]:
+            nc.vector.tensor_tensor(by_slate(result[:, cols]), by_slate(shifted[:, cols]), per_slate(minus_log, cols),
+                                    ALU.add)
             nc.sync.dma_start(out[:, cols], result[:, cols])
+        cols = pieces[0]
+        for first in range(cols.start, cols.stop, SLATE):
+            entries = slice(first, first + SLATE)
+            nc.scalar.activation(result[:, entries], shifted[:, entries], ACT.Identity,
+                                 bias=minus_log[:, first // SLATE:first // SLATE + 1])
+        nc.scalar.dma_start(out[:, cols], result[:, cols])

import math

import concourse.mybir as mybir

BF16, F32, U16, U32 = mybir.dt.bfloat16, mybir.dt.float32, mybir.dt.uint16, mybir.dt.uint32
ALU = mybir.AluOpType
ACT = mybir.ActivationFunctionType
AXIS_X = mybir.AxisListType.X

FLOPS = 2 * 128 * 128 * 1024

SLATE = 16
BATCHES = (((0, 256), (256, 512)), ((512, 768),), ((768, 1024),))

LN2 = math.log(2.0)
GAP = math.log(1.0 / LN2) - (1.0 / LN2 - 1.0) * LN2
GUESS_SCALE = LN2 / 2.0 ** 23
GUESS_BIAS = GAP / 2 - 127 * LN2


def tile_rows_slate_logpr_rep_kernel(tc, table, w, r, offs, out):
    nc = tc.nc
    K, S = table.shape
    M, N = out.shape
    with (
        tc.tile_pool(name="held", bufs=1) as held,
        tc.psum_pool(name="psum", bufs=1) as psum,
    ):
        table_sb = held.tile([K, S], BF16)
        w_sb = held.tile([K, M], BF16)
        offsets = held.tile([128, N // 16], U16)
        r_twice = held.tile([2, N], F32)
        nc.sync.dma_start(table_sb[:], table)
        nc.sync.dma_start(offsets[:], offs)
        nc.scalar.dma_start(w_sb[:], w)
        nc.scalar.dma_start(r_twice[:], r[0].partition_broadcast(2))

        add_two_rows = held.tile([K, M], BF16)
        nc.vector.memset(add_two_rows[:], 0.0)
        nc.scalar.activation(add_two_rows[0:2, :], add_two_rows[0:2, :], ACT.Exp)
        r_parts = held.tile([K, N], BF16)
        nc.vector.memset(r_parts[:], 0.0)
        take_off = held.tile([2, 1], F32)
        nc.vector.memset(take_off[:], -1.0)
        nc.vector.memset(take_off[0:1, :], 0.0)
        r_rounded = held.tile([2, N], BF16)
        pieces = [slice(*piece) for batch in BATCHES for piece in batch]
        for cols in pieces:
            if cols.start == 0:
                nc.vector.tensor_copy(r_rounded[:, cols], r_twice[:, cols])
            else:
                nc.scalar.activation(r_rounded[:, cols], r_twice[:, cols], ACT.Copy)
            nc.vector.scalar_tensor_tensor(r_parts[0:2, cols], r_rounded[:, cols], take_off[:], r_twice[:, cols],
                                           ALU.mult, ALU.add)

        banks = {cols.start: psum.tile([M, cols.stop - cols.start], F32, name="scores%d" % cols.start) for cols in pieces}
        for cols in pieces:
            entries = offsets[:, cols.start // 16:cols.stop // 16]
            nc.tensor.matmul(banks[cols.start][:], w_sb[:], table_sb[:].indirect(entries), start=True, stop=False)
        for cols in pieces:
            nc.tensor.matmul(banks[cols.start][:], add_two_rows[:], r_parts[:, cols], start=False, stop=True)

        def by_slate(values):
            return values.rearrange("p (v t) -> p v t", t=SLATE)

        def per_slate(stat, cols):
            values = stat[:, cols.start // SLATE:cols.stop // SLATE]
            return values.unsqueeze(2).to_broadcast([M, (cols.stop - cols.start) // SLATE, SLATE])

        top = held.tile([M, N // SLATE], F32)
        shifted = held.tile([M, N], F32)
        exps = held.tile([M, N], F32)
        total = held.tile([M, N // SLATE], F32)
        inverse = held.tile([M, N // SLATE], F32)
        guess = held.tile([M, N // SLATE], F32)
        ratio = held.tile([M, N // SLATE], F32)
        parabola = held.tile([M, N // SLATE], F32)
        minus_log = held.tile([M, N // SLATE], F32)
        result = held.tile([M, N], F32)
        for cols in pieces:
            slates = slice(cols.start // SLATE, cols.stop // SLATE)
            scores = by_slate(banks[cols.start][:])
            nc.vector.tensor_reduce(top[:, slates], scores, AXIS_X, ALU.max)
            nc.vector.tensor_tensor(by_slate(shifted[:, cols]), scores, per_slate(top, cols), ALU.subtract)
            nc.scalar.activation(exps[:, cols], shifted[:, cols], ACT.Exp)

        for batch in BATCHES:
            cols = slice(batch[0][0], batch[-1][1])
            slates = slice(cols.start // SLATE, cols.stop // SLATE)
            nc.vector.tensor_reduce(total[:, slates], by_slate(exps[:, cols]), AXIS_X, ALU.add)
            bits = total[:, slates].bitcast(U32)
            nc.scalar.activation(inverse[:, slates], bits, ACT.Exp, scale=-GUESS_SCALE, bias=-GUESS_BIAS)
            nc.scalar.activation(guess[:, slates], bits, ACT.Copy, scale=GUESS_SCALE, bias=GUESS_BIAS - 1.5)
            nc.vector.tensor_tensor(ratio[:, slates], total[:, slates], inverse[:, slates], ALU.mult)
            nc.vector.scalar_tensor_tensor(parabola[:, slates], ratio[:, slates], -4.0, ratio[:, slates], ALU.add, ALU.mult)
            nc.vector.scalar_tensor_tensor(minus_log[:, slates], parabola[:, slates], 0.5, guess[:, slates],
                                           ALU.mult, ALU.subtract)

        for cols in pieces[1:]:
            nc.vector.tensor_tensor(by_slate(result[:, cols]), by_slate(shifted[:, cols]), per_slate(minus_log, cols),
                                    ALU.add)
            nc.sync.dma_start(out[:, cols], result[:, cols])
        cols = pieces[0]
        for first in range(cols.start, cols.stop, SLATE):
            entries = slice(first, first + SLATE)
            nc.scalar.activation(result[:, entries], shifted[:, entries], ACT.Identity,
                                 bias=minus_log[:, first // SLATE:first // SLATE + 1])
        nc.scalar.dma_start(out[:, cols], result[:, cols])
